import numpy as np
import ml_dtypes


def mxq(x, axis, fmt="e4m3"):
    dtype, down = {"e4m3": (ml_dtypes.float8_e4m3fn, 7), "e5m2": (ml_dtypes.float8_e5m2, 14)}[fmt]
    v = np.moveaxis(np.asarray(x, np.float32).astype(ml_dtypes.bfloat16).astype(np.float64), axis, -1)
    blocks = v.reshape(v.shape[:-1] + (-1, 32))
    amax = np.abs(blocks).max(-1, keepdims=True)
    byte = np.maximum(np.where(amax > 0, np.frexp(amax)[1] - 1 + 127, 0) - down, 1)
    scale = np.exp2(byte - 127.0)
    codes = (blocks / scale).astype(np.float32).astype(dtype).astype(np.float64)
    return np.moveaxis((codes * scale).reshape(v.shape), -1, axis)


WIDE = False


def mx_kscale(k):
    if not WIDE:
        return np.ones(k)
    levels = np.array([10, -10, 5, -5, 0])
    if k % 512:
        return np.exp2(np.random.permutation(np.resize(levels, k // 32))).repeat(32)
    a = np.empty((k // 512, 16))
    for p in range(k // 512):
        a[p, :8] = np.random.permutation(np.resize(levels, 8))
        for g in range(8):
            far = levels[np.abs(levels - a[p, g]) >= 10]
            a[p, g + 8] = far[np.random.randint(len(far))]
    return np.exp2(a.ravel()).repeat(32)


def f64(x):
    return np.asarray(x).astype(np.float64)


def striped(idx):
    return np.tile(idx.reshape(-1, 16).T, (8, 1)).astype(np.uint16)


def unstriped(offs):
    return offs[:16].T.reshape(-1).astype(np.int64)


E2M1 = np.array([0.0, 0.5, 1.0, 1.5, 2.0, 3.0, 4.0, 6.0, -0.0, -0.5, -1.0, -1.5, -2.0, -3.0, -4.0, -6.0])


def pack_weight(w, fmt):
    k, n = w.shape
    w = f64(np.asarray(w, np.float32).astype(ml_dtypes.bfloat16)).reshape(k // 32, 32, n)
    amax = np.abs(w).max(1)
    if fmt == "e4m3":
        byte = np.frexp(amax)[1] - 1 + 127 - 7
    else:
        mant, ex = np.frexp(amax / 6.0)
        byte = np.where(mant > 0.5, ex, ex - 1) + 127
    byte = np.clip(np.where(amax > 0, byte, 1), 1, 254)
    scaled = (w * np.exp2(127.0 - byte)[:, None, :]).reshape(k, n).astype(np.float32)
    by_word = np.ascontiguousarray(scaled.reshape(k // 512, 128, 4, n).transpose(0, 1, 3, 2))
    if fmt == "e4m3":
        words = by_word.astype(ml_dtypes.float8_e4m3fn).view(np.uint8)
    else:
        c = by_word.astype(ml_dtypes.float4_e2m1fn).view(np.uint8) & 0xF
        words = (c[..., 0::2] | (c[..., 1::2] << 4)).reshape(k // 512, 128, 2 * n)
    return np.ascontiguousarray(words), np.ascontiguousarray(byte.astype(np.uint8).reshape(k // 512, 16, n))


def unpack_weight(words, scales, fmt):
    g, _, n = scales.shape
    words = np.ascontiguousarray(words).reshape(g, 128, n, -1)
    if fmt == "e4m3":
        vals = words.view(ml_dtypes.float8_e4m3fn).astype(np.float64)
    else:
        nib = np.empty((g, 128, n, 4), np.uint8)
        nib[..., 0::2] = words & 0xF
        nib[..., 1::2] = words >> 4
        vals = E2M1[nib]
    vals = vals * np.repeat(np.exp2(scales.astype(np.float64) - 127.0), 8, axis=1)[..., None]
    return vals.transpose(0, 1, 3, 2).reshape(g * 512, n)


def gelu(v):
    return 0.5 * v * (1.0 + np.tanh(np.sqrt(2.0 / np.pi) * (v + 0.044715 * v**3)))


K, H, N, S, T = 1024, 1024, 512, 512, 4096


def setup_inputs():
    n = np.random.standard_normal
    s = mx_kscale(K)[:, None]
    u = mx_kscale(H)[:, None]
    tab_words, tab_scales = pack_weight(n((K, T)) * s, "e4m3")
    w3_words, w3_scales = pack_weight(n((K, H)) / s / np.sqrt(K), "e2m1")
    w5_words, w5_scales = pack_weight(0.7 * n((K, N)) / s / np.sqrt(K), "e4m3")
    return {
        "tab_words": tab_words, "tab_scales": tab_scales,
        "offs": striped(np.random.permutation(T)[:S]),
        "offs2": striped(np.random.permutation(T)[:S]),
        "offs3": striped(np.random.permutation(T)[:S]),
        "w1": (n((K, H)) * u.T / s / np.sqrt(K)).astype(np.float32),
        "w2": (n((K, H)) * u.T / s / np.sqrt(K)).astype(np.float32),
        "w3_words": w3_words, "w3_scales": w3_scales,
        "phase": np.random.uniform(1.4, 2.8, H).astype(np.float32),
        "w4": (1.2 * n((H, N)) / u / np.sqrt(H)).astype(np.float32),
        "w5_words": w5_words, "w5_scales": w5_scales,
        "bias": (0.5 * n(N)).astype(np.float32),
    }


def reference(tab_words, tab_scales, offs, offs2, offs3, w1, w2, w3_words, w3_scales, phase, w4, w5_words, w5_scales, bias):
    TW = unpack_weight(tab_words, tab_scales, "e4m3")
    v = TW[:, unstriped(offs)]
    v2 = TW[:, unstriped(offs2)]
    v3 = TW[:, unstriped(offs3)]
    a = mxq(f64(w1), 0, "e4m3").T @ v
    b = mxq(f64(w2), 0, "e4m3").T @ v2
    d = unpack_weight(w3_words, w3_scales, "e2m1").T @ v3
    h = np.minimum(a, b) * np.sin(f64(phase)[:, None] * np.tanh(d))
    hq = mxq(h, 0, "e4m3")
    w4q = mxq(f64(w4), 0, "e4m3")
    w5 = unpack_weight(w5_words, w5_scales, "e4m3")
    y = w4q.T @ hq + w5.T @ v
    return np.tanh(y + f64(bias)[:, None])

@@ -1,0 +1,329 @@
+from contextlib import ExitStack
+
+import concourse.mybir as mybir
+from concourse.masks import make_identity
+
+K, H, N, S, T = 1024, 1024, 512, 512, 4096
+FLOPS = 2 * S * (3 * K * H + H * N + K * N)
+
+F32 = mybir.dt.float32
+BF16 = mybir.dt.bfloat16
+I32 = mybir.dt.int32
+U32 = mybir.dt.uint32
+U16 = mybir.dt.uint16
+U8 = mybir.dt.uint8
+FP8X4 = mybir.dt.float8_e4m3fn_x4
+FP4X4 = mybir.dt.float4_e2m1fn_x4
+ACT = mybir.ActivationFunctionType
+ALU = mybir.AluOpType
+
+P = 128
+PACK = 4
+KP = P * PACK
+PASSES = K // KP
+HALVES = H // KP
+QUADS = 4
+JC = 128
+CHUNKS = S // JC
+NT = N // P
+LAST_SPLIT = 20
+BIAS_ROW = 32
+
+
+def tile_list_bid_rigging_alarms_kernel(
+    tc, tab_words, tab_scales, offs, offs2, offs3, w1, w2, w3_words, w3_scales, phase, w4, w5_words, w5_scales, bias, out
+):
+    nc = tc.nc
+    with ExitStack() as ctx:
+        keep = ctx.enter_context(tc.tile_pool(name="keep", bufs=1))
+        ring = ctx.enter_context(tc.tile_pool(name="ring", bufs=3))
+        psum = ctx.enter_context(tc.psum_pool(name="psum", bufs=4))
+
+        def kept(shape, dtype, name):
+            return keep.tile(shape, dtype, name=name, tag=name, align_bytes=64)
+
+
+        rows_raw = kept([BIAS_ROW + 1, KP], F32, "rows_raw")
+        nc.scalar.dma_start(out=rows_raw[0:HALVES, :], in_=phase.rearrange("(b r) -> b r", b=HALVES))
+        nc.scalar.dma_start(out=rows_raw[BIAS_ROW : BIAS_ROW + 1, :], in_=bias.rearrange("(o n) -> o n", o=1))
+
+        scale_rows = kept([P, T], U8, "scale_rows")
+        nc.sync.dma_start(
+            out=scale_rows[0:32, :].bitcast(I32), in_=tab_scales.rearrange("a q t -> (a q) t").bitcast(I32)
+        )
+        nc.vector.memset(scale_rows[32:64, :].bitcast(I32), 0)
+        nc.vector.memset(scale_rows[64:128, :].bitcast(I32), 0)
+        lists = {}
+        for key, src in (("tender", offs3), ("bidder", offs), ("rival", offs2)):
+            lists[key] = keep.tile([P, S // 16], U16, name=f"list_{key}")
+            nc.sync.dma_start(lists[key][:], src)
+        order = ("tender", "bidder", "rival")
+
+        table = []
+        for a in range(PASSES):
+            table.append(kept([P, T], I32, f"table{a}"))
+            nc.sync.dma_start(out=table[a][:], in_=tab_words[a].rearrange("p t i -> p (t i)").bitcast(I32))
+
+        w3s_raw = kept([P, PASSES, H], U8, "w3s_raw")
+        nc.gpsimd.memset(w3s_raw[:].rearrange("p a c -> p (a c)").bitcast(I32), 0)
+        for q in range(QUADS):
+            nc.gpsimd.dma_start(
+                out=w3s_raw[32 * q : 32 * q + 4, :, :].bitcast(I32),
+                in_=w3_scales[:, 4 * q : 4 * q + 4, :].rearrange("a r c -> r a c").bitcast(I32),
+            )
+        planes = kept([P, PASSES, 3 * S], U8, "planes")
+        nc.gpsimd.memset(planes[:].rearrange("p a c -> p (a c)").bitcast(I32), 0)
+        rows = kept([P, KP], F32, "rows")
+        nc.gpsimd.memset(rows[:], 0.0)
+        ident = kept([P, P], F32, "ident")
+        make_identity(nc, ident[:])
+        w5s = kept([P, PASSES, N], U8, "w5s")
+        nc.gpsimd.memset(w5s[:].rearrange("p a c -> p (a c)").bitcast(I32), 0)
+        w3s = kept([P, PASSES, H], U8, "w3s")
+
+        picked_scales = kept([P, 3 * S], U8, "picked_scales")
+        for u, key in enumerate(order):
+            nc.vector.tensor_copy(picked_scales[:, u * S : (u + 1) * S], scale_rows[:].indirect(lists[key][:]))
+
+        def carry_scales(a):
+            for q in range(QUADS):
+                r0 = 16 * a + 4 * q
+                nc.sync.dma_start(
+                    out=planes[32 * q : 32 * q + 4, a, :].bitcast(I32), in_=picked_scales[r0 : r0 + 4, :].bitcast(I32)
+                )
+
+        carry_scales(0)
+        w3_raw = kept([P, PASSES, H // 2], I32, "w3_raw")
+        nc.sync.dma_start(out=w3_raw[:], in_=w3_words.rearrange("a p c -> p a c").bitcast(I32))
+        carry_scales(1)
+
+        raw = {}
+
+        def load_first_stage(key, w, a, b):
+            raw[key, a, b] = kept([P, PACK, KP], F32, f"raw_{key}{a}{b}")
+            nc.sync.dma_start(
+                out=raw[key, a, b][:],
+                in_=w[a * KP : (a + 1) * KP, b * KP : (b + 1) * KP].rearrange("(p j) c -> p j c", j=PACK),
+            )
+
+        for b in range(HALVES):
+            for key, w in (("w1", w1), ("w2", w2)):
+                for a in range(PASSES):
+                    load_first_stage(key, w, a, b)
+            if b == 0:
+                for q in range(QUADS):
+                    nc.sync.dma_start(
+                        out=w5s[32 * q : 32 * q + 4, :, :].bitcast(I32),
+                        in_=w5_scales[:, 4 * q : 4 * q + 4, :].rearrange("a r c -> r a c").bitcast(I32),
+                    )
+        for b in range(HALVES):
+            raw["w4", b] = kept([P, PACK, N], F32, f"raw_w4{b}")
+            w4_rows = w4[b * KP : (b + 1) * KP, :].rearrange("(c t i) n -> t c i n", t=PACK, i=4)
+            for t in range(PACK):
+                nc.sync.dma_start(out=raw["w4", b][:, t, :], in_=w4_rows[t])
+        w5 = kept([P, PASSES, N], U32, "w5")
+        nc.sync.dma_start(out=w5[:].bitcast(I32), in_=w5_words.rearrange("a p n i -> p a (n i)").bitcast(I32))
+
+        nc.scalar.copy(
+            out=rows[0:HALVES, :].rearrange("b (t c i) -> b c t i", t=PACK, i=4),
+            in_=rows_raw[0:HALVES, :].rearrange("b (c t i) -> b c t i", t=PACK, i=4),
+        )
+        nc.scalar.copy(out=rows[BIAS_ROW : BIAS_ROW + 1, :], in_=rows_raw[BIAS_ROW : BIAS_ROW + 1, :])
+        turned = psum.tile([P, PACK, P], F32, name="turned", tag="z")
+        for g in range(PACK):
+            nc.tensor.transpose(turned[:, g, :], rows[:, g * P : (g + 1) * P], ident[:])
+        consts = kept([P, PACK, BIAS_ROW + 1], F32, "consts")
+        nc.scalar.copy(out=consts[:], in_=turned[:, :, 0 : BIAS_ROW + 1])
+
+        picked = {}
+        for a in range(PASSES):
+            for key in order:
+                picked[key, a] = kept([P, S], U32, f"picked_{key}{a}")
+                nc.vector.tensor_copy(picked[key, a][:], table[a][:].bitcast(U32).indirect(lists[key][:]))
+
+        def moving(key, a, j0, width):
+            c0 = order.index(key) * S + j0
+            return dict(
+                rhs=picked[key, a][:, j0 : j0 + width].bitcast(FP8X4), rhs_scale=planes[:, a, c0 : c0 + width]
+            )
+
+        nc.scalar.copy(
+            out=w3s[:].rearrange("p a c -> p (a c)").bitcast(U32).rearrange("p (g t c) -> p g c t", t=PACK, c=32),
+            in_=w3s_raw[:].rearrange("p a c -> p (a c)").bitcast(U32).rearrange("p (g c t) -> p g c t", t=PACK, c=32),
+        )
+        w3 = []
+        for b in range(HALVES):
+            w3.append(kept([P, PASSES, 2 * KP], U8, f"w3_{b}"))
+            nc.scalar.copy(
+                out=w3[b][:].bitcast(U32).rearrange("p a (t c e) -> p a c t e", t=PACK, e=2),
+                in_=w3_raw[:, :, b * 256 : (b + 1) * 256].bitcast(U32).rearrange("p a (c t e) -> p a c t e", t=PACK, e=2),
+            )
+        sines = [kept([P, PACK, S], F32, f"sines{b}") for b in range(HALVES)]
+        for b in range(HALVES):
+            for t in range(PACK):
+                d = psum.tile([P, S], F32, name="d", tag="xz"[b])
+                for a in range(PASSES):
+                    nc.tensor.matmul_mx(
+                        out=d[:],
+                        lhsT=w3[b][:, a, 2 * P * t : 2 * P * (t + 1)].bitcast(FP4X4),
+                        lhsT_scale=w3s[:, a, b * KP + t * P : b * KP + (t + 1) * P],
+                        start=(a == 0),
+                        stop=(a == PASSES - 1),
+                        **moving("tender", a, 0, S),
+                    )
+                nc.scalar.activation(out=sines[b][:, t, :], in_=d[:], func=ACT.Tanh)
+
+        def take_sines(b):
+            for t in range(PACK):
+                nc.scalar.activation(
+                    out=sines[b][:, t, :], in_=sines[b][:, t, :], func=ACT.Sin, scale=consts[:, t, b : b + 1]
+                )
+
+        grouped, codes, scales = {}, {}, {}
+
+        def round_first_stage(key, a, b, shares):
+            grouped[key, a, b] = ring.tile([P, PACK * KP], BF16, name="grouped", align_bytes=64)
+            dst = grouped[key, a, b][:].rearrange("p (t c i j) -> p c t j i", t=PACK, i=4, j=PACK)
+            src = raw[key, a, b][:].rearrange("p j (c t i) -> p c t j i", t=PACK, i=4)
+            for copy, c0, c1 in shares:
+                copy(out=dst[:, c0:c1], in_=src[:, c0:c1])
+
+        def quantise(key):
+            label = "".join(str(part) for part in key)
+            width = grouped[key].shape[1] // PACK
+            codes[key] = kept([P, width], U32, f"codes_{label}")
+            scales[key] = kept([P, width], U8, f"scales_{label}")
+            nc.vector.quantize_mx(out=codes[key][:].bitcast(FP8X4), scales=scales[key][:], in_=grouped[key][:])
+
+        def stationary(key, m):
+            cols = slice(m * P, (m + 1) * P)
+            return dict(lhsT=codes[key][:, cols].bitcast(FP8X4), lhsT_scale=scales[key][:, cols])
+
+        on_vector = [(nc.vector.tensor_copy, 0, 32)]
+        on_scalar = [(nc.scalar.copy, 0, 32)]
+
+        bidder_all = keep.tile([P, HALVES, PACK, S], F32, name="bidder", tag="table1", align_bytes=64)
+        bidder = [bidder_all[:, b] for b in range(HALVES)]
+
+        def first_products(b):
+            for t in range(PACK):
+                acc = psum.tile([P, S], F32, name="acc", tag="z")
+                for a in range(PASSES):
+                    nc.tensor.matmul_mx(
+                        out=acc[:],
+                        start=(a == 0),
+                        stop=(a == PASSES - 1),
+                        **stationary(("w1", a, b), t),
+                        **moving("bidder", a, 0, S),
+                    )
+                nc.scalar.copy(out=bidder[b][:, t, :], in_=acc[:])
+
+        rival = {}
+
+        def rival_pass(a, b):
+            for jc in range(CHUNKS):
+                if a == 0:
+                    rival[b, jc] = psum.tile([P, PACK, JC], F32, name="rival", tag="x")
+                for t in range(PACK):
+                    nc.tensor.matmul_mx(
+                        out=rival[b, jc][:, t, :],
+                        start=(a == 0 and t == 0),
+                        stop=(a == PASSES - 1 and t == PACK - 1),
+                        **stationary(("w2", a, b), t),
+                        **moving("rival", a, jc * JC, JC),
+                    )
+
+        smaller = {}
+
+        def take_min(b, jc):
+            smaller[b, jc] = ring.tile([P, PACK, JC], F32, name="smaller")
+            nc.vector.tensor_tensor(
+                out=smaller[b, jc][:], in0=bidder[b][:, :, jc * JC : (jc + 1) * JC], in1=rival[b, jc][:], op=ALU.min
+            )
+
+        def modulate(b, jc):
+            grouped["h", b, jc] = ring.tile([P, PACK * JC], BF16, name="h_grouped", align_bytes=64)
+            nc.vector.tensor_tensor(
+                out=grouped["h", b, jc][:].rearrange("p (c i t) -> p c t i", i=4, t=PACK),
+                in0=smaller[b, jc][:].rearrange("p t (c i) -> p c t i", i=4),
+                in1=sines[b][:, :, jc * JC : (jc + 1) * JC].rearrange("p t (c i) -> p c t i", i=4),
+                op=ALU.mult,
+            )
+
+        def make_h(b):
+            for step in range(CHUNKS + 2):
+                if step < CHUNKS:
+                    take_min(b, step)
+                if 1 <= step <= CHUNKS:
+                    modulate(b, step - 1)
+                if step >= 2:
+                    quantise(("h", b, step - 2))
+
+        def round_w4(b):
+            grouped["w4", b] = ring.tile([P, PACK * N], BF16, name="grouped", align_bytes=64)
+            nc.scalar.copy(
+                out=grouped["w4", b][:].rearrange("p (c i t) -> p c t i", i=4, t=PACK),
+                in_=raw["w4", b][:].rearrange("p t (c i) -> p c t i", i=4),
+            )
+
+        take_sines(0)
+        for a in range(PASSES):
+            round_first_stage("w1", a, 0, on_vector)
+            quantise(("w1", a, 0))
+        first_products(0)
+        take_sines(1)
+        for a in range(PASSES):
+            round_first_stage("w2", a, 0, on_vector)
+            quantise(("w2", a, 0))
+            rival_pass(a, 0)
+        for a in range(PASSES):
+            round_first_stage("w1", a, 1, on_scalar)
+            quantise(("w1", a, 1))
+        make_h(0)
+        round_first_stage("w2", 0, 1, on_scalar)
+        first_products(1)
+        round_first_stage("w2", 1, 1, on_vector)
+        for a in range(PASSES):
+            quantise(("w2", a, 1))
+            rival_pass(a, 1)
+        for b in range(HALVES):
+            round_w4(b)
+            quantise(("w4", b))
+        make_h(1)
+
+        score = [psum.tile([P, NT, JC], F32, name=f"score{jc}", tag="z") for jc in range(CHUNKS)]
+
+        def h_pass(b, jc, start, stop):
+            key = ("h", b, jc)
+            for m in range(NT):
+                nc.tensor.matmul_mx(
+                    out=score[jc][:, m, :],
+                    rhs=codes[key][:].bitcast(FP8X4),
+                    rhs_scale=scales[key][:],
+                    start=(start and m == 0),
+                    stop=(stop and m == NT - 1),
+                    **stationary(("w4", b), m),
+                )
+
+        for jc in range(CHUNKS):
+            h_pass(0, jc, True, False)
+        for jc in range(CHUNKS):
+            for a in range(PASSES):
+                for m in range(NT):
+                    nc.tensor.matmul_mx(
+                        out=score[jc][:, m, :],
+                        lhsT=w5[:, a, m * P : (m + 1) * P].bitcast(FP8X4),
+                        lhsT_scale=w5s[:, a, m * P : (m + 1) * P],
+                        start=False,
+                        stop=False,
+                        **moving("bidder", a, jc * JC, JC),
+                    )
+        alarm = keep.tile([P, CHUNKS, NT, JC], F32, name="alarm", tag="table0", align_bytes=64)
+        out_rows = out.rearrange("(m p) j -> p m j", p=P)
+        for jc in range(CHUNKS):
+            h_pass(1, jc, False, True)
+            for m in range(NT):
+                nc.scalar.activation(
+                    out=alarm[:, jc, m, :], in_=score[jc][:, m, :], func=ACT.Tanh, bias=consts[:, m, BIAS_ROW : BIAS_ROW + 1]
+                )
+            nc.sync.dma_start(out=out_rows[:, :, jc * JC : (jc + 1) * JC], in_=alarm[:, jc])

@@ -28,6 +28,8 @@ CHUNKS = S // JC
 NT = N // P
 LAST_SPLIT = 20
 BIAS_ROW = 32
+ROW_STEP = 28
+WIDE = 256
 
 
 def tile_list_bid_rigging_alarms_kernel(
@@ -44,33 +46,38 @@ def tile_list_bid_rigging_alarms_kernel(
 
 
         rows_raw = kept([BIAS_ROW + 1, KP], F32, "rows_raw")
-        nc.scalar.dma_start(out=rows_raw[0:HALVES, :], in_=phase.rearrange("(b r) -> b r", b=HALVES))
-        nc.scalar.dma_start(out=rows_raw[BIAS_ROW : BIAS_ROW + 1, :], in_=bias.rearrange("(o n) -> o n", o=1))
+        nc.sync.dma_start(out=rows_raw[0:HALVES, :], in_=phase.rearrange("(b r) -> b r", b=HALVES))
+        nc.sync.dma_start(out=rows_raw[BIAS_ROW : BIAS_ROW + 1, :], in_=bias.rearrange("(o n) -> o n", o=1))
 
         scale_rows = kept([P, T], U8, "scale_rows")
-        nc.sync.dma_start(
-            out=scale_rows[0:32, :].bitcast(I32), in_=tab_scales.rearrange("a q t -> (a q) t").bitcast(I32)
-        )
-        nc.vector.memset(scale_rows[32:64, :].bitcast(I32), 0)
-        nc.vector.memset(scale_rows[64:128, :].bitcast(I32), 0)
+        nc.vector.memset(scale_rows[:].bitcast(I32), 0)
+        w3s_raw = kept([P, PASSES, H], U8, "w3s_raw")
+        nc.vector.memset(w3s_raw[:].rearrange("p a c -> p (a c)").bitcast(I32), 0)
         lists = {}
         for key, src in (("tender", offs3), ("bidder", offs), ("rival", offs2)):
             lists[key] = keep.tile([P, S // 16], U16, name=f"list_{key}")
             nc.sync.dma_start(lists[key][:], src)
+        for a in range(PASSES):
+            nc.sync.dma_start(
+                out=scale_rows[ROW_STEP * a : ROW_STEP * a + 16, :].bitcast(I32), in_=tab_scales[a].bitcast(I32)
+            )
         order = ("tender", "bidder", "rival")
 
-        table = []
-        for a in range(PASSES):
-            table.append(kept([P, T], I32, f"table{a}"))
+        table = [kept([P, T], I32, f"table{a}") for a in range(PASSES)]
+
+        def load_table(a):
             nc.sync.dma_start(out=table[a][:], in_=tab_words[a].rearrange("p t i -> p (t i)").bitcast(I32))
 
-        w3s_raw = kept([P, PASSES, H], U8, "w3s_raw")
-        nc.gpsimd.memset(w3s_raw[:].rearrange("p a c -> p (a c)").bitcast(I32), 0)
+        load_table(0)
         for q in range(QUADS):
-            nc.gpsimd.dma_start(
+            nc.sync.dma_start(
                 out=w3s_raw[32 * q : 32 * q + 4, :, :].bitcast(I32),
                 in_=w3_scales[:, 4 * q : 4 * q + 4, :].rearrange("a r c -> r a c").bitcast(I32),
             )
+        w3_raw = kept([P, PASSES, H // 2], I32, "w3_raw")
+        nc.sync.dma_start(out=w3_raw[:], in_=w3_words.rearrange("a p c -> p a c").bitcast(I32))
+        load_table(1)
+
         planes = kept([P, PASSES, 3 * S], U8, "planes")
         nc.gpsimd.memset(planes[:].rearrange("p a c -> p (a c)").bitcast(I32), 0)
         rows = kept([P, KP], F32, "rows")
@@ -85,17 +92,11 @@ def tile_list_bid_rigging_alarms_kernel(
         for u, key in enumerate(order):
             nc.vector.tensor_copy(picked_scales[:, u * S : (u + 1) * S], scale_rows[:].indirect(lists[key][:]))
 
-        def carry_scales(a):
+        for a in range(PASSES):
             for q in range(QUADS):
-                r0 = 16 * a + 4 * q
-                nc.sync.dma_start(
-                    out=planes[32 * q : 32 * q + 4, a, :].bitcast(I32), in_=picked_scales[r0 : r0 + 4, :].bitcast(I32)
-                )
-
-        carry_scales(0)
-        w3_raw = kept([P, PASSES, H // 2], I32, "w3_raw")
-        nc.sync.dma_start(out=w3_raw[:], in_=w3_words.rearrange("a p c -> p a c").bitcast(I32))
-        carry_scales(1)
+                r0 = ROW_STEP * a + 4 * q
+                carry = nc.vector.tensor_copy if r0 == 32 * q else nc.sync.dma_start
+                carry(planes[32 * q : 32 * q + 4, a, :].bitcast(I32), picked_scales[r0 : r0 + 4, :].bitcast(I32))
 
         raw = {}
 
@@ -159,19 +160,29 @@ def tile_list_bid_rigging_alarms_kernel(
                 in_=w3_raw[:, :, b * 256 : (b + 1) * 256].bitcast(U32).rearrange("p a (c t e) -> p a c t e", t=PACK, e=2),
             )
         sines = [kept([P, PACK, S], F32, f"sines{b}") for b in range(HALVES)]
-        for b in range(HALVES):
-            for t in range(PACK):
-                d = psum.tile([P, S], F32, name="d", tag="xz"[b])
-                for a in range(PASSES):
-                    nc.tensor.matmul_mx(
-                        out=d[:],
-                        lhsT=w3[b][:, a, 2 * P * t : 2 * P * (t + 1)].bitcast(FP4X4),
-                        lhsT_scale=w3s[:, a, b * KP + t * P : b * KP + (t + 1) * P],
-                        start=(a == 0),
-                        stop=(a == PASSES - 1),
-                        **moving("tender", a, 0, S),
-                    )
-                nc.scalar.activation(out=sines[b][:, t, :], in_=d[:], func=ACT.Tanh)
+        d = {}
+
+        def tender_pass(a, b, t):
+            if a == 0:
+                d[b, t] = psum.tile([P, S], F32, name="d", tag="xz"[b])
+            nc.tensor.matmul_mx(
+                out=d[b, t][:],
+                lhsT=w3[b][:, a, 2 * P * t : 2 * P * (t + 1)].bitcast(FP4X4),
+                lhsT_scale=w3s[:, a, b * KP + t * P : b * KP + (t + 1) * P],
+                start=(a == 0),
+                stop=(a == PASSES - 1),
+                **moving("tender", a, 0, S),
+            )
+            if a == PASSES - 1:
+                nc.scalar.activation(out=sines[b][:, t, :], in_=d[b, t][:], func=ACT.Tanh)
+
+        for t in range(PACK):
+            tender_pass(0, 0, t)
+        for t in range(PACK):
+            tender_pass(1, 0, t)
+            tender_pass(0, 1, t)
+        for t in range(PACK):
+            tender_pass(1, 1, t)
 
         def take_sines(b):
             for t in range(PACK):
@@ -259,11 +270,11 @@ def tile_list_bid_rigging_alarms_kernel(
                 if step >= 2:
                     quantise(("h", b, step - 2))
 
-        def round_w4(b):
-            grouped["w4", b] = ring.tile([P, PACK * N], BF16, name="grouped", align_bytes=64)
+        def round_w4(b, nh):
+            grouped["w4", b, nh] = ring.tile([P, PACK * WIDE], BF16, name="w4_grouped", align_bytes=64)
             nc.scalar.copy(
-                out=grouped["w4", b][:].rearrange("p (c i t) -> p c t i", i=4, t=PACK),
-                in_=raw["w4", b][:].rearrange("p t (c i) -> p c t i", i=4),
+                out=grouped["w4", b, nh][:].rearrange("p (c i t) -> p c t i", i=4, t=PACK),
+                in_=raw["w4", b][:, :, nh * WIDE : (nh + 1) * WIDE].rearrange("p t (c i) -> p c t i", i=4),
             )
 
         take_sines(0)
@@ -277,7 +288,7 @@ def tile_list_bid_rigging_alarms_kernel(
             quantise(("w2", a, 0))
             rival_pass(a, 0)
         for a in range(PASSES):
-            round_first_stage("w1", a, 1, on_scalar)
+            round_first_stage("w1", a, 1, on_scalar if a else on_vector)
             quantise(("w1", a, 1))
         make_h(0)
         round_first_stage("w2", 0, 1, on_scalar)
@@ -287,43 +298,62 @@ def tile_list_bid_rigging_alarms_kernel(
             quantise(("w2", a, 1))
             rival_pass(a, 1)
         for b in range(HALVES):
-            round_w4(b)
-            quantise(("w4", b))
+            for nh in range(2):
+                round_w4(b, nh)
+                quantise(("w4", b, nh))
         make_h(1)
 
-        score = [psum.tile([P, NT, JC], F32, name=f"score{jc}", tag="z") for jc in range(CHUNKS)]
+        score = {}
+        for jh in range(2):
+            for nh in range(2):
+                score[nh, jh] = psum.tile([P, 2, WIDE], F32, name="score", tag="z")
 
-        def h_pass(b, jc, start, stop):
+        def h_pass(b, jc, nh):
+            jh, second = divmod(jc, 2)
             key = ("h", b, jc)
-            for m in range(NT):
+            for m in range(2):
                 nc.tensor.matmul_mx(
-                    out=score[jc][:, m, :],
+                    out=score[nh, jh][:, m, second * JC : (second + 1) * JC],
                     rhs=codes[key][:].bitcast(FP8X4),
                     rhs_scale=scales[key][:],
-                    start=(start and m == 0),
-                    stop=(stop and m == NT - 1),
-                    **stationary(("w4", b), m),
+                    start=(b == 0 and second == 0 and m == 0),
+                    stop=(b == 1 and second == 1 and m == 1),
+                    **stationary(("w4", b, nh), m),
                 )
 
-        for jc in range(CHUNKS):
-            h_pass(0, jc, True, False)
-        for jc in range(CHUNKS):
-            for a in range(PASSES):
-                for m in range(NT):
+        def own_passes(jh, nh):
+            for m in range(2):
+                cols = slice((2 * nh + m) * P, (2 * nh + m + 1) * P)
+                for a in range(PASSES):
                     nc.tensor.matmul_mx(
-                        out=score[jc][:, m, :],
-                        lhsT=w5[:, a, m * P : (m + 1) * P].bitcast(FP8X4),
-                        lhsT_scale=w5s[:, a, m * P : (m + 1) * P],
+                        out=score[nh, jh][:, m, :],
+                        lhsT=w5[:, a, cols].bitcast(FP8X4),
+                        lhsT_scale=w5s[:, a, cols],
                         start=False,
                         stop=False,
-                        **moving("bidder", a, jc * JC, JC),
+                        **moving("bidder", a, jh * WIDE, WIDE),
                     )
-        alarm = keep.tile([P, CHUNKS, NT, JC], F32, name="alarm", tag="table0", align_bytes=64)
+
+        for nh in range(2):
+            for jc in range(CHUNKS):
+                h_pass(0, jc, nh)
+        alarm = keep.tile([P, 2, NT, WIDE], F32, name="alarm", tag="table0", align_bytes=64)
         out_rows = out.rearrange("(m p) j -> p m j", p=P)
-        for jc in range(CHUNKS):
-            h_pass(1, jc, False, True)
-            for m in range(NT):
-                nc.scalar.activation(
-                    out=alarm[:, jc, m, :], in_=score[jc][:, m, :], func=ACT.Tanh, bias=consts[:, m, BIAS_ROW : BIAS_ROW + 1]
+        for jh in range(2):
+            for nh in range(2):
+                own_passes(jh, nh)
+                h_pass(1, 2 * jh, nh)
+            for nh in range(2):
+                h_pass(1, 2 * jh + 1, nh)
+                for m in range(2):
+                    n = 2 * nh + m
+                    nc.scalar.activation(
+                        out=alarm[:, jh, n, :],
+                        in_=score[nh, jh][:, m, :],
+                        func=ACT.Tanh,
+                        bias=consts[:, n, BIAS_ROW : BIAS_ROW + 1],
+                    )
+                nc.sync.dma_start(
+                    out=out_rows[:, 2 * nh : 2 * nh + 2, jh * WIDE : (jh + 1) * WIDE],
+                    in_=alarm[:, jh, 2 * nh : 2 * nh + 2, :],
                 )
-            nc.sync.dma_start(out=out_rows[:, :, jc * JC : (jc + 1) * JC], in_=alarm[:, jc])

@@ -26,9 +26,8 @@ QUADS = 4
 JC = 128
 CHUNKS = S // JC
 NT = N // P
-LAST_SPLIT = 20
 BIAS_ROW = 32
-ROW_STEP = 28
+SCALE_RUNS = ((0, 0, 4, 0), (1, 0, 2, 28), (1, 2, 4, 64))
 WIDE = 256
 
 
@@ -45,10 +44,6 @@ def tile_list_bid_rigging_alarms_kernel(
             return keep.tile(shape, dtype, name=name, tag=name, align_bytes=64)
 
 
-        rows_raw = kept([BIAS_ROW + 1, KP], F32, "rows_raw")
-        nc.sync.dma_start(out=rows_raw[0:HALVES, :], in_=phase.rearrange("(b r) -> b r", b=HALVES))
-        nc.sync.dma_start(out=rows_raw[BIAS_ROW : BIAS_ROW + 1, :], in_=bias.rearrange("(o n) -> o n", o=1))
-
         scale_rows = kept([P, T], U8, "scale_rows")
         nc.vector.memset(scale_rows[:].bitcast(I32), 0)
         w3s_raw = kept([P, PASSES, H], U8, "w3s_raw")
@@ -57,10 +52,14 @@ def tile_list_bid_rigging_alarms_kernel(
         for key, src in (("tender", offs3), ("bidder", offs), ("rival", offs2)):
             lists[key] = keep.tile([P, S // 16], U16, name=f"list_{key}")
             nc.sync.dma_start(lists[key][:], src)
-        for a in range(PASSES):
+        home = {}
+        for a, q0, q1, first in SCALE_RUNS:
             nc.sync.dma_start(
-                out=scale_rows[ROW_STEP * a : ROW_STEP * a + 16, :].bitcast(I32), in_=tab_scales[a].bitcast(I32)
+                out=scale_rows[first : first + 4 * (q1 - q0), :].bitcast(I32),
+                in_=tab_scales[a, 4 * q0 : 4 * q1, :].bitcast(I32),
             )
+            for q in range(q0, q1):
+                home[a, q] = first + 4 * (q - q0)
         order = ("tender", "bidder", "rival")
 
         table = [kept([P, T], I32, f"table{a}") for a in range(PASSES)]
@@ -69,13 +68,15 @@ def tile_list_bid_rigging_alarms_kernel(
             nc.sync.dma_start(out=table[a][:], in_=tab_words[a].rearrange("p t i -> p (t i)").bitcast(I32))
 
         load_table(0)
+        rows_raw = kept([BIAS_ROW + 1, KP], F32, "rows_raw")
+        nc.sync.dma_start(out=rows_raw[0:HALVES, :], in_=phase.rearrange("(b r) -> b r", b=HALVES))
+        nc.sync.dma_start(out=rows_raw[BIAS_ROW : BIAS_ROW + 1, :], in_=bias.rearrange("(o n) -> o n", o=1))
+
         for q in range(QUADS):
             nc.sync.dma_start(
                 out=w3s_raw[32 * q : 32 * q + 4, :, :].bitcast(I32),
                 in_=w3_scales[:, 4 * q : 4 * q + 4, :].rearrange("a r c -> r a c").bitcast(I32),
             )
-        w3_raw = kept([P, PASSES, H // 2], I32, "w3_raw")
-        nc.sync.dma_start(out=w3_raw[:], in_=w3_words.rearrange("a p c -> p a c").bitcast(I32))
         load_table(1)
 
         planes = kept([P, PASSES, 3 * S], U8, "planes")
@@ -94,9 +95,12 @@ def tile_list_bid_rigging_alarms_kernel(
 
         for a in range(PASSES):
             for q in range(QUADS):
-                r0 = ROW_STEP * a + 4 * q
+                r0 = home[a, q]
                 carry = nc.vector.tensor_copy if r0 == 32 * q else nc.sync.dma_start
                 carry(planes[32 * q : 32 * q + 4, a, :].bitcast(I32), picked_scales[r0 : r0 + 4, :].bitcast(I32))
+
+        w3_raw = kept([P, PASSES, H // 2], I32, "w3_raw")
+        nc.sync.dma_start(out=w3_raw[:], in_=w3_words.rearrange("a p c -> p a c").bitcast(I32))
 
         raw = {}
 
@@ -107,11 +111,11 @@ def tile_list_bid_rigging_alarms_kernel(
                 in_=w[a * KP : (a + 1) * KP, b * KP : (b + 1) * KP].rearrange("(p j) c -> p j c", j=PACK),
             )
 
-        for b in range(HALVES):
-            for key, w in (("w1", w1), ("w2", w2)):
-                for a in range(PASSES):
-                    load_first_stage(key, w, a, b)
-            if b == 0:
+        weights = {"w1": w1, "w2": w2}
+        arrival = [("w1", 0, 0), ("w1", 1, 0), ("w2", 0, 0), ("w1", 0, 1), ("w2", 1, 0), ("w1", 1, 1), ("w2", 0, 1), ("w2", 1, 1)]
+        for n, (key, a, b) in enumerate(arrival):
+            load_first_stage(key, weights[key], a, b)
+            if n == 3:
                 for q in range(QUADS):
                     nc.sync.dma_start(
                         out=w5s[32 * q : 32 * q + 4, :, :].bitcast(I32),
@@ -160,29 +164,19 @@ def tile_list_bid_rigging_alarms_kernel(
                 in_=w3_raw[:, :, b * 256 : (b + 1) * 256].bitcast(U32).rearrange("p a (c t e) -> p a c t e", t=PACK, e=2),
             )
         sines = [kept([P, PACK, S], F32, f"sines{b}") for b in range(HALVES)]
-        d = {}
-
-        def tender_pass(a, b, t):
-            if a == 0:
-                d[b, t] = psum.tile([P, S], F32, name="d", tag="xz"[b])
-            nc.tensor.matmul_mx(
-                out=d[b, t][:],
-                lhsT=w3[b][:, a, 2 * P * t : 2 * P * (t + 1)].bitcast(FP4X4),
-                lhsT_scale=w3s[:, a, b * KP + t * P : b * KP + (t + 1) * P],
-                start=(a == 0),
-                stop=(a == PASSES - 1),
-                **moving("tender", a, 0, S),
-            )
-            if a == PASSES - 1:
-                nc.scalar.activation(out=sines[b][:, t, :], in_=d[b, t][:], func=ACT.Tanh)
-
-        for t in range(PACK):
-            tender_pass(0, 0, t)
-        for t in range(PACK):
-            tender_pass(1, 0, t)
-            tender_pass(0, 1, t)
-        for t in range(PACK):
-            tender_pass(1, 1, t)
+        for b in range(HALVES):
+            for t in range(PACK):
+                d = psum.tile([P, S], F32, name="d", tag="xz"[b])
+                for a in range(PASSES):
+                    nc.tensor.matmul_mx(
+                        out=d[:],
+                        lhsT=w3[b][:, a, 2 * P * t : 2 * P * (t + 1)].bitcast(FP4X4),
+                        lhsT_scale=w3s[:, a, b * KP + t * P : b * KP + (t + 1) * P],
+                        start=(a == 0),
+                        stop=(a == PASSES - 1),
+                        **moving("tender", a, 0, S),
+                    )
+                nc.scalar.activation(out=sines[b][:, t, :], in_=d[:], func=ACT.Tanh)
 
         def take_sines(b):
             for t in range(PACK):
@@ -192,15 +186,15 @@ def tile_list_bid_rigging_alarms_kernel(
 
         grouped, codes, scales = {}, {}, {}
 
-        def round_first_stage(key, a, b, shares):
-            grouped[key, a, b] = ring.tile([P, PACK * KP], BF16, name="grouped", align_bytes=64)
-            dst = grouped[key, a, b][:].rearrange("p (t c i j) -> p c t j i", t=PACK, i=4, j=PACK)
-            src = raw[key, a, b][:].rearrange("p j (c t i) -> p c t j i", t=PACK, i=4)
-            for copy, c0, c1 in shares:
-                copy(out=dst[:, c0:c1], in_=src[:, c0:c1])
+        def round_first_stage(key, a, b, u, copy):
+            grouped[key, a, b, u] = ring.tile([P, 2 * KP], BF16, name="grouped", bufs=6, align_bytes=64)
+            copy(
+                out=grouped[key, a, b, u][:].rearrange("p (t c i j) -> p c t j i", t=2, i=4, j=PACK),
+                in_=raw[key, a, b][:].rearrange("p j (c t i) -> p c t j i", t=PACK, i=4)[:, :, 2 * u : 2 * u + 2],
+            )
 
         def quantise(key):
-            label = "".join(str(part) for part in key)
+            label = len(codes)
             width = grouped[key].shape[1] // PACK
             codes[key] = kept([P, width], U32, f"codes_{label}")
             scales[key] = kept([P, width], U8, f"scales_{label}")
@@ -210,8 +204,11 @@ def tile_list_bid_rigging_alarms_kernel(
             cols = slice(m * P, (m + 1) * P)
             return dict(lhsT=codes[key][:, cols].bitcast(FP8X4), lhsT_scale=scales[key][:, cols])
 
-        on_vector = [(nc.vector.tensor_copy, 0, 32)]
-        on_scalar = [(nc.scalar.copy, 0, 32)]
+        def prepare(key, copy):
+            for u in range(2):
+                round_first_stage(*key, u, copy)
+            for u in range(2):
+                quantise((*key, u))
 
         bidder_all = keep.tile([P, HALVES, PACK, S], F32, name="bidder", tag="table1", align_bytes=64)
         bidder = [bidder_all[:, b] for b in range(HALVES)]
@@ -224,7 +221,7 @@ def tile_list_bid_rigging_alarms_kernel(
                         out=acc[:],
                         start=(a == 0),
                         stop=(a == PASSES - 1),
-                        **stationary(("w1", a, b), t),
+                        **stationary(("w1", a, b, t // 2), t % 2),
                         **moving("bidder", a, 0, S),
                     )
                 nc.scalar.copy(out=bidder[b][:, t, :], in_=acc[:])
@@ -240,63 +237,70 @@ def tile_list_bid_rigging_alarms_kernel(
                         out=rival[b, jc][:, t, :],
                         start=(a == 0 and t == 0),
                         stop=(a == PASSES - 1 and t == PACK - 1),
-                        **stationary(("w2", a, b), t),
+                        **stationary(("w2", a, b, t // 2), t % 2),
                         **moving("rival", a, jc * JC, JC),
                     )
 
+        pieces = {0: [(0, 2), (2, 4)], 1: [(0, 2), (2, 3), (3, 4)]}
         smaller = {}
 
-        def take_min(b, jc):
-            smaller[b, jc] = ring.tile([P, PACK, JC], F32, name="smaller")
-            nc.vector.tensor_tensor(
-                out=smaller[b, jc][:], in0=bidder[b][:, :, jc * JC : (jc + 1) * JC], in1=rival[b, jc][:], op=ALU.min
-            )
+        def take_min(b, piece):
+            j0, j1 = piece
+            smaller[b, piece] = ring.tile([P, PACK, (j1 - j0) * JC], F32, name="smaller")
+            for jc in range(j0, j1):
+                nc.vector.tensor_tensor(
+                    out=smaller[b, piece][:, :, (jc - j0) * JC : (jc - j0 + 1) * JC],
+                    in0=bidder[b][:, :, jc * JC : (jc + 1) * JC],
+                    in1=rival[b, jc][:],
+                    op=ALU.min,
+                )
 
-        def modulate(b, jc):
-            grouped["h", b, jc] = ring.tile([P, PACK * JC], BF16, name="h_grouped", align_bytes=64)
+        def modulate(b, piece):
+            j0, j1 = piece
+            grouped["h", b, piece] = ring.tile([P, PACK * (j1 - j0) * JC], BF16, name="h_grouped", align_bytes=64)
             nc.vector.tensor_tensor(
-                out=grouped["h", b, jc][:].rearrange("p (c i t) -> p c t i", i=4, t=PACK),
-                in0=smaller[b, jc][:].rearrange("p t (c i) -> p c t i", i=4),
-                in1=sines[b][:, :, jc * JC : (jc + 1) * JC].rearrange("p t (c i) -> p c t i", i=4),
+                out=grouped["h", b, piece][:].rearrange("p (c i t) -> p c t i", i=4, t=PACK),
+                in0=smaller[b, piece][:].rearrange("p t (c i) -> p c t i", i=4),
+                in1=sines[b][:, :, j0 * JC : j1 * JC].rearrange("p t (c i) -> p c t i", i=4),
                 op=ALU.mult,
             )
 
         def make_h(b):
-            for step in range(CHUNKS + 2):
-                if step < CHUNKS:
-                    take_min(b, step)
-                if 1 <= step <= CHUNKS:
-                    modulate(b, step - 1)
+            count = len(pieces[b])
+            for step in range(count + 2):
+                if step < count:
+                    take_min(b, pieces[b][step])
+                if 1 <= step <= count:
+                    modulate(b, pieces[b][step - 1])
                 if step >= 2:
-                    quantise(("h", b, step - 2))
+                    quantise(("h", b, pieces[b][step - 2]))
 
         def round_w4(b, nh):
-            grouped["w4", b, nh] = ring.tile([P, PACK * WIDE], BF16, name="w4_grouped", align_bytes=64)
+            grouped["w4", b, nh] = ring.tile([P, PACK * WIDE], BF16, name="grouped", bufs=6, align_bytes=64)
             nc.scalar.copy(
                 out=grouped["w4", b, nh][:].rearrange("p (c i t) -> p c t i", i=4, t=PACK),
                 in_=raw["w4", b][:, :, nh * WIDE : (nh + 1) * WIDE].rearrange("p t (c i) -> p c t i", i=4),
             )
 
         take_sines(0)
-        for a in range(PASSES):
-            round_first_stage("w1", a, 0, on_vector)
-            quantise(("w1", a, 0))
+        for key in arrival[0:2]:
+            prepare(key, nc.vector.tensor_copy)
         first_products(0)
         take_sines(1)
-        for a in range(PASSES):
-            round_first_stage("w2", a, 0, on_vector)
-            quantise(("w2", a, 0))
-            rival_pass(a, 0)
-        for a in range(PASSES):
-            round_first_stage("w1", a, 1, on_scalar if a else on_vector)
-            quantise(("w1", a, 1))
-        make_h(0)
-        round_first_stage("w2", 0, 1, on_scalar)
+        for key in arrival[2:5]:
+            prepare(key, nc.vector.tensor_copy)
+            if key[0] == "w2":
+                rival_pass(key[1], 0)
+        for key in arrival[5:7]:
+            prepare(key, nc.scalar.copy)
+        round_first_stage(*arrival[7], 1, nc.scalar.copy)
         first_products(1)
-        round_first_stage("w2", 1, 1, on_vector)
-        for a in range(PASSES):
-            quantise(("w2", a, 1))
-            rival_pass(a, 1)
+        make_h(0)
+        rival_pass(0, 1)
+        round_first_stage(*arrival[7], 0, nc.vector.tensor_copy)
+        for u in range(2):
+            quantise((*arrival[7], u))
+        rival_pass(1, 1)
         for b in range(HALVES):
             for nh in range(2):
                 round_w4(b, nh)
@@ -308,16 +312,17 @@ def tile_list_bid_rigging_alarms_kernel(
             for nh in range(2):
                 score[nh, jh] = psum.tile([P, 2, WIDE], F32, name="score", tag="z")
 
-        def h_pass(b, jc, nh):
-            jh, second = divmod(jc, 2)
-            key = ("h", b, jc)
+        def h_pass(b, piece, nh):
+            j0, j1 = piece
+            jh = j0 // 2
+            key = ("h", b, piece)
             for m in range(2):
                 nc.tensor.matmul_mx(
-                    out=score[nh, jh][:, m, second * JC : (second + 1) * JC],
+                    out=score[nh, jh][:, m, (j0 - 2 * jh) * JC : (j1 - 2 * jh) * JC],
                     rhs=codes[key][:].bitcast(FP8X4),
                     rhs_scale=scales[key][:],
-                    start=(b == 0 and second == 0 and m == 0),
-                    stop=(b == 1 and second == 1 and m == 1),
+                    start=(b == 0 and m == 0),
+                    stop=(b == 1 and j1 % 2 == 0 and m == 1),
                     **stationary(("w4", b, nh), m),
                 )
 
@@ -335,16 +340,18 @@ def tile_list_bid_rigging_alarms_kernel(
                     )
 
         for nh in range(2):
-            for jc in range(CHUNKS):
-                h_pass(0, jc, nh)
+            for piece in pieces[0]:
+                h_pass(0, piece, nh)
         alarm = keep.tile([P, 2, NT, WIDE], F32, name="alarm", tag="table0", align_bytes=64)
         out_rows = out.rearrange("(m p) j -> p m j", p=P)
         for jh in range(2):
+            mine = [piece for piece in pieces[1] if piece[0] // 2 == jh]
             for nh in range(2):
                 own_passes(jh, nh)
-                h_pass(1, 2 * jh, nh)
+                for piece in mine[:-1]:
+                    h_pass(1, piece, nh)
             for nh in range(2):
-                h_pass(1, 2 * jh + 1, nh)
+                h_pass(1, mine[-1], nh)
                 for m in range(2):
                     n = 2 * nh + m
                     nc.scalar.activation(

@@ -43,6 +43,9 @@ def tile_list_bid_rigging_alarms_kernel(
         def kept(shape, dtype, name):
             return keep.tile(shape, dtype, name=name, tag=name, align_bytes=64)
 
+        warm = kept([P, 2], F32, "warm")
+        nc.vector.memset(warm[:, 0:1], 0.0)
+        nc.scalar.activation(out=warm[:, 1:2], in_=warm[:, 0:1], func=ACT.Silu)
 
         scale_rows = kept([P, T], U8, "scale_rows")
         nc.vector.memset(scale_rows[:].bitcast(I32), 0)

from contextlib import ExitStack

import concourse.mybir as mybir
from concourse.masks import make_identity

K, H, N, S, T = 1024, 1024, 512, 512, 4096
FLOPS = 2 * S * (3 * K * H + H * N + K * N)

F32 = mybir.dt.float32
BF16 = mybir.dt.bfloat16
I32 = mybir.dt.int32
U32 = mybir.dt.uint32
U16 = mybir.dt.uint16
U8 = mybir.dt.uint8
FP8X4 = mybir.dt.float8_e4m3fn_x4
FP4X4 = mybir.dt.float4_e2m1fn_x4
ACT = mybir.ActivationFunctionType
ALU = mybir.AluOpType

P = 128
PACK = 4
KP = P * PACK
PASSES = K // KP
HALVES = H // KP
QUADS = 4
JC = 128
CHUNKS = S // JC
NT = N // P
BIAS_ROW = 32
SCALE_RUNS = ((0, 0, 4, 0), (1, 0, 2, 28), (1, 2, 4, 64))
WIDE = 256


def tile_list_bid_rigging_alarms_kernel(
    tc, tab_words, tab_scales, offs, offs2, offs3, w1, w2, w3_words, w3_scales, phase, w4, w5_words, w5_scales, bias, out
):
    nc = tc.nc
    with ExitStack() as ctx:
        keep = ctx.enter_context(tc.tile_pool(name="keep", bufs=1))
        ring = ctx.enter_context(tc.tile_pool(name="ring", bufs=3))
        psum = ctx.enter_context(tc.psum_pool(name="psum", bufs=4))

        def kept(shape, dtype, name):
            return keep.tile(shape, dtype, name=name, tag=name, align_bytes=64)

        warm = kept([P, 2], F32, "warm")
        nc.vector.memset(warm[:, 0:1], 0.0)
        nc.scalar.activation(out=warm[:, 1:2], in_=warm[:, 0:1], func=ACT.Silu)

        scale_rows = kept([P, T], U8, "scale_rows")
        nc.vector.memset(scale_rows[:].bitcast(I32), 0)
        w3s_raw = kept([P, PASSES, H], U8, "w3s_raw")
        nc.vector.memset(w3s_raw[:].rearrange("p a c -> p (a c)").bitcast(I32), 0)
        lists = {}
        for key, src in (("tender", offs3), ("bidder", offs), ("rival", offs2)):
            lists[key] = keep.tile([P, S // 16], U16, name=f"list_{key}")
            nc.sync.dma_start(lists[key][:], src)
        home = {}
        for a, q0, q1, first in SCALE_RUNS:
            nc.sync.dma_start(
                out=scale_rows[first : first + 4 * (q1 - q0), :].bitcast(I32),
                in_=tab_scales[a, 4 * q0 : 4 * q1, :].bitcast(I32),
            )
            for q in range(q0, q1):
                home[a, q] = first + 4 * (q - q0)
        order = ("tender", "bidder", "rival")

        table = [kept([P, T], I32, f"table{a}") for a in range(PASSES)]

        def load_table(a):
            nc.sync.dma_start(out=table[a][:], in_=tab_words[a].rearrange("p t i -> p (t i)").bitcast(I32))

        load_table(0)
        rows_raw = kept([BIAS_ROW + 1, KP], F32, "rows_raw")
        nc.sync.dma_start(out=rows_raw[0:HALVES, :], in_=phase.rearrange("(b r) -> b r", b=HALVES))
        nc.sync.dma_start(out=rows_raw[BIAS_ROW : BIAS_ROW + 1, :], in_=bias.rearrange("(o n) -> o n", o=1))

        for q in range(QUADS):
            nc.sync.dma_start(
                out=w3s_raw[32 * q : 32 * q + 4, :, :].bitcast(I32),
                in_=w3_scales[:, 4 * q : 4 * q + 4, :].rearrange("a r c -> r a c").bitcast(I32),
            )
        load_table(1)

        planes = kept([P, PASSES, 3 * S], U8, "planes")
        nc.gpsimd.memset(planes[:].rearrange("p a c -> p (a c)").bitcast(I32), 0)
        rows = kept([P, KP], F32, "rows")
        nc.gpsimd.memset(rows[:], 0.0)
        ident = kept([P, P], F32, "ident")
        make_identity(nc, ident[:])
        w5s = kept([P, PASSES, N], U8, "w5s")
        nc.gpsimd.memset(w5s[:].rearrange("p a c -> p (a c)").bitcast(I32), 0)
        w3s = kept([P, PASSES, H], U8, "w3s")

        picked_scales = kept([P, 3 * S], U8, "picked_scales")
        for u, key in enumerate(order):
            nc.vector.tensor_copy(picked_scales[:, u * S : (u + 1) * S], scale_rows[:].indirect(lists[key][:]))

        for a in range(PASSES):
            for q in range(QUADS):
                r0 = home[a, q]
                carry = nc.vector.tensor_copy if r0 == 32 * q else nc.sync.dma_start
                carry(planes[32 * q : 32 * q + 4, a, :].bitcast(I32), picked_scales[r0 : r0 + 4, :].bitcast(I32))

        w3_raw = kept([P, PASSES, H // 2], I32, "w3_raw")
        nc.sync.dma_start(out=w3_raw[:], in_=w3_words.rearrange("a p c -> p a c").bitcast(I32))

        raw = {}

        def load_first_stage(key, w, a, b):
            raw[key, a, b] = kept([P, PACK, KP], F32, f"raw_{key}{a}{b}")
            nc.sync.dma_start(
                out=raw[key, a, b][:],
                in_=w[a * KP : (a + 1) * KP, b * KP : (b + 1) * KP].rearrange("(p j) c -> p j c", j=PACK),
            )

        weights = {"w1": w1, "w2": w2}
        arrival = [("w1", 0, 0), ("w1", 1, 0), ("w2", 0, 0), ("w1", 0, 1), ("w2", 1, 0), ("w1", 1, 1), ("w2", 0, 1), ("w2", 1, 1)]
        for n, (key, a, b) in enumerate(arrival):
            load_first_stage(key, weights[key], a, b)
            if n == 3:
                for q in range(QUADS):
                    nc.sync.dma_start(
                        out=w5s[32 * q : 32 * q + 4, :, :].bitcast(I32),
                        in_=w5_scales[:, 4 * q : 4 * q + 4, :].rearrange("a r c -> r a c").bitcast(I32),
                    )
        for b in range(HALVES):
            raw["w4", b] = kept([P, PACK, N], F32, f"raw_w4{b}")
            w4_rows = w4[b * KP : (b + 1) * KP, :].rearrange("(c t i) n -> t c i n", t=PACK, i=4)
            for t in range(PACK):
                nc.sync.dma_start(out=raw["w4", b][:, t, :], in_=w4_rows[t])
        w5 = kept([P, PASSES, N], U32, "w5")
        nc.sync.dma_start(out=w5[:].bitcast(I32), in_=w5_words.rearrange("a p n i -> p a (n i)").bitcast(I32))

        nc.scalar.copy(
            out=rows[0:HALVES, :].rearrange("b (t c i) -> b c t i", t=PACK, i=4),
            in_=rows_raw[0:HALVES, :].rearrange("b (c t i) -> b c t i", t=PACK, i=4),
        )
        nc.scalar.copy(out=rows[BIAS_ROW : BIAS_ROW + 1, :], in_=rows_raw[BIAS_ROW : BIAS_ROW + 1, :])
        turned = psum.tile([P, PACK, P], F32, name="turned", tag="z")
        for g in range(PACK):
            nc.tensor.transpose(turned[:, g, :], rows[:, g * P : (g + 1) * P], ident[:])
        consts = kept([P, PACK, BIAS_ROW + 1], F32, "consts")
        nc.scalar.copy(out=consts[:], in_=turned[:, :, 0 : BIAS_ROW + 1])

        picked = {}
        for a in range(PASSES):
            for key in order:
                picked[key, a] = kept([P, S], U32, f"picked_{key}{a}")
                nc.vector.tensor_copy(picked[key, a][:], table[a][:].bitcast(U32).indirect(lists[key][:]))

        def moving(key, a, j0, width):
            c0 = order.index(key) * S + j0
            return dict(
                rhs=picked[key, a][:, j0 : j0 + width].bitcast(FP8X4), rhs_scale=planes[:, a, c0 : c0 + width]
            )

        nc.scalar.copy(
            out=w3s[:].rearrange("p a c -> p (a c)").bitcast(U32).rearrange("p (g t c) -> p g c t", t=PACK, c=32),
            in_=w3s_raw[:].rearrange("p a c -> p (a c)").bitcast(U32).rearrange("p (g c t) -> p g c t", t=PACK, c=32),
        )
        w3 = []
        for b in range(HALVES):
            w3.append(kept([P, PASSES, 2 * KP], U8, f"w3_{b}"))
            nc.scalar.copy(
                out=w3[b][:].bitcast(U32).rearrange("p a (t c e) -> p a c t e", t=PACK, e=2),
                in_=w3_raw[:, :, b * 256 : (b + 1) * 256].bitcast(U32).rearrange("p a (c t e) -> p a c t e", t=PACK, e=2),
            )
        sines = [kept([P, PACK, S], F32, f"sines{b}") for b in range(HALVES)]
        for b in range(HALVES):
            for t in range(PACK):
                d = psum.tile([P, S], F32, name="d", tag="xz"[b])
                for a in range(PASSES):
                    nc.tensor.matmul_mx(
                        out=d[:],
                        lhsT=w3[b][:, a, 2 * P * t : 2 * P * (t + 1)].bitcast(FP4X4),
                        lhsT_scale=w3s[:, a, b * KP + t * P : b * KP + (t + 1) * P],
                        start=(a == 0),
                        stop=(a == PASSES - 1),
                        **moving("tender", a, 0, S),
                    )
                nc.scalar.activation(out=sines[b][:, t, :], in_=d[:], func=ACT.Tanh)

        def take_sines(b):
            for t in range(PACK):
                nc.scalar.activation(
                    out=sines[b][:, t, :], in_=sines[b][:, t, :], func=ACT.Sin, scale=consts[:, t, b : b + 1]
                )

        grouped, codes, scales = {}, {}, {}

        def round_first_stage(key, a, b, u, copy):
            grouped[key, a, b, u] = ring.tile([P, 2 * KP], BF16, name="grouped", bufs=6, align_bytes=64)
            copy(
                out=grouped[key, a, b, u][:].rearrange("p (t c i j) -> p c t j i", t=2, i=4, j=PACK),
                in_=raw[key, a, b][:].rearrange("p j (c t i) -> p c t j i", t=PACK, i=4)[:, :, 2 * u : 2 * u + 2],
            )

        def quantise(key):
            label = len(codes)
            width = grouped[key].shape[1] // PACK
            codes[key] = kept([P, width], U32, f"codes_{label}")
            scales[key] = kept([P, width], U8, f"scales_{label}")
            nc.vector.quantize_mx(out=codes[key][:].bitcast(FP8X4), scales=scales[key][:], in_=grouped[key][:])

        def stationary(key, m):
            cols = slice(m * P, (m + 1) * P)
            return dict(lhsT=codes[key][:, cols].bitcast(FP8X4), lhsT_scale=scales[key][:, cols])

        def prepare(key, copy):
            for u in range(2):
                round_first_stage(*key, u, copy)
            for u in range(2):
                quantise((*key, u))

        bidder_all = keep.tile([P, HALVES, PACK, S], F32, name="bidder", tag="table1", align_bytes=64)
        bidder = [bidder_all[:, b] for b in range(HALVES)]

        def first_products(b):
            for t in range(PACK):
                acc = psum.tile([P, S], F32, name="acc", tag="z")
                for a in range(PASSES):
                    nc.tensor.matmul_mx(
                        out=acc[:],
                        start=(a == 0),
                        stop=(a == PASSES - 1),
                        **stationary(("w1", a, b, t // 2), t % 2),
                        **moving("bidder", a, 0, S),
                    )
                nc.scalar.copy(out=bidder[b][:, t, :], in_=acc[:])

        rival = {}

        def rival_pass(a, b):
            for jc in range(CHUNKS):
                if a == 0:
                    rival[b, jc] = psum.tile([P, PACK, JC], F32, name="rival", tag="x")
                for t in range(PACK):
                    nc.tensor.matmul_mx(
                        out=rival[b, jc][:, t, :],
                        start=(a == 0 and t == 0),
                        stop=(a == PASSES - 1 and t == PACK - 1),
                        **stationary(("w2", a, b, t // 2), t % 2),
                        **moving("rival", a, jc * JC, JC),
                    )

        pieces = {0: [(0, 2), (2, 4)], 1: [(0, 2), (2, 3), (3, 4)]}
        smaller = {}

        def take_min(b, piece):
            j0, j1 = piece
            smaller[b, piece] = ring.tile([P, PACK, (j1 - j0) * JC], F32, name="smaller")
            for jc in range(j0, j1):
                nc.vector.tensor_tensor(
                    out=smaller[b, piece][:, :, (jc - j0) * JC : (jc - j0 + 1) * JC],
                    in0=bidder[b][:, :, jc * JC : (jc + 1) * JC],
                    in1=rival[b, jc][:],
                    op=ALU.min,
                )

        def modulate(b, piece):
            j0, j1 = piece
            grouped["h", b, piece] = ring.tile([P, PACK * (j1 - j0) * JC], BF16, name="h_grouped", align_bytes=64)
            nc.vector.tensor_tensor(
                out=grouped["h", b, piece][:].rearrange("p (c i t) -> p c t i", i=4, t=PACK),
                in0=smaller[b, piece][:].rearrange("p t (c i) -> p c t i", i=4),
                in1=sines[b][:, :, j0 * JC : j1 * JC].rearrange("p t (c i) -> p c t i", i=4),
                op=ALU.mult,
            )

        def make_h(b):
            count = len(pieces[b])
            for step in range(count + 2):
                if step < count:
                    take_min(b, pieces[b][step])
                if 1 <= step <= count:
                    modulate(b, pieces[b][step - 1])
                if step >= 2:
                    quantise(("h", b, pieces[b][step - 2]))

        def round_w4(b, nh):
            grouped["w4", b, nh] = ring.tile([P, PACK * WIDE], BF16, name="grouped", bufs=6, align_bytes=64)
            nc.scalar.copy(
                out=grouped["w4", b, nh][:].rearrange("p (c i t) -> p c t i", i=4, t=PACK),
                in_=raw["w4", b][:, :, nh * WIDE : (nh + 1) * WIDE].rearrange("p t (c i) -> p c t i", i=4),
            )

        take_sines(0)
        for key in arrival[0:2]:
            prepare(key, nc.vector.tensor_copy)
        first_products(0)
        take_sines(1)
        for key in arrival[2:5]:
            prepare(key, nc.vector.tensor_copy)
            if key[0] == "w2":
                rival_pass(key[1], 0)
        for key in arrival[5:7]:
            prepare(key, nc.scalar.copy)
        round_first_stage(*arrival[7], 1, nc.scalar.copy)
        first_products(1)
        make_h(0)
        rival_pass(0, 1)
        round_first_stage(*arrival[7], 0, nc.vector.tensor_copy)
        for u in range(2):
            quantise((*arrival[7], u))
        rival_pass(1, 1)
        for b in range(HALVES):
            for nh in range(2):
                round_w4(b, nh)
                quantise(("w4", b, nh))
        make_h(1)

        score = {}
        for jh in range(2):
            for nh in range(2):
                score[nh, jh] = psum.tile([P, 2, WIDE], F32, name="score", tag="z")

        def h_pass(b, piece, nh):
            j0, j1 = piece
            jh = j0 // 2
            key = ("h", b, piece)
            for m in range(2):
                nc.tensor.matmul_mx(
                    out=score[nh, jh][:, m, (j0 - 2 * jh) * JC : (j1 - 2 * jh) * JC],
                    rhs=codes[key][:].bitcast(FP8X4),
                    rhs_scale=scales[key][:],
                    start=(b == 0 and m == 0),
                    stop=(b == 1 and j1 % 2 == 0 and m == 1),
                    **stationary(("w4", b, nh), m),
                )

        def own_passes(jh, nh):
            for m in range(2):
                cols = slice((2 * nh + m) * P, (2 * nh + m + 1) * P)
                for a in range(PASSES):
                    nc.tensor.matmul_mx(
                        out=score[nh, jh][:, m, :],
                        lhsT=w5[:, a, cols].bitcast(FP8X4),
                        lhsT_scale=w5s[:, a, cols],
                        start=False,
                        stop=False,
                        **moving("bidder", a, jh * WIDE, WIDE),
                    )

        for nh in range(2):
            for piece in pieces[0]:
                h_pass(0, piece, nh)
        alarm = keep.tile([P, 2, NT, WIDE], F32, name="alarm", tag="table0", align_bytes=64)
        out_rows = out.rearrange("(m p) j -> p m j", p=P)
        for jh in range(2):
            mine = [piece for piece in pieces[1] if piece[0] // 2 == jh]
            for nh in range(2):
                own_passes(jh, nh)
                for piece in mine[:-1]:
                    h_pass(1, piece, nh)
            for nh in range(2):
                h_pass(1, mine[-1], nh)
                for m in range(2):
                    n = 2 * nh + m
                    nc.scalar.activation(
                        out=alarm[:, jh, n, :],
                        in_=score[nh, jh][:, m, :],
                        func=ACT.Tanh,
                        bias=consts[:, n, BIAS_ROW : BIAS_ROW + 1],
                    )
                nc.sync.dma_start(
                    out=out_rows[:, 2 * nh : 2 * nh + 2, jh * WIDE : (jh + 1) * WIDE],
                    in_=alarm[:, jh, 2 * nh : 2 * nh + 2, :],
                )
